import numpy as np
import ml_dtypes


def mxq(x, axis, fmt="e4m3"):
    dtype, down = {"e4m3": (ml_dtypes.float8_e4m3fn, 7), "e5m2": (ml_dtypes.float8_e5m2, 14)}[fmt]
    v = np.moveaxis(np.asarray(x, np.float32).astype(ml_dtypes.bfloat16).astype(np.float64), axis, -1)
    blocks = v.reshape(v.shape[:-1] + (-1, 32))
    amax = np.abs(blocks).max(-1, keepdims=True)
    byte = np.maximum(np.where(amax > 0, np.frexp(amax)[1] - 1 + 127, 0) - down, 1)
    scale = np.exp2(byte - 127.0)
    codes = (blocks / scale).astype(np.float32).astype(dtype).astype(np.float64)
    return np.moveaxis((codes * scale).reshape(v.shape), -1, axis)


WIDE = False


def mx_kscale(k):
    if not WIDE:
        return np.ones(k)
    levels = np.array([10, -10, 5, -5, 0])
    if k % 512:
        return np.exp2(np.random.permutation(np.resize(levels, k // 32))).repeat(32)
    a = np.empty((k // 512, 16))
    for p in range(k // 512):
        a[p, :8] = np.random.permutation(np.resize(levels, 8))
        for g in range(8):
            far = levels[np.abs(levels - a[p, g]) >= 10]
            a[p, g + 8] = far[np.random.randint(len(far))]
    return np.exp2(a.ravel()).repeat(32)


def f64(x):
    return np.asarray(x).astype(np.float64)


def striped(idx):
    return np.tile(idx.reshape(-1, 16).T, (8, 1)).astype(np.uint16)


def unstriped(offs):
    return offs[:16].T.reshape(-1).astype(np.int64)


def striped8(idx):
    return np.concatenate([x.reshape(-1, 16).T for x in idx]).astype(np.uint16)


def runs(offs, k):
    lists = np.stack([offs[16 * r : 16 * r + 16].T.reshape(-1) for r in range(8)]).astype(np.int64)
    return lists[np.arange(k) % 512 // 64]


def pack_weight(w):
    k, n = w.shape
    w = f64(np.asarray(w, np.float32).astype(ml_dtypes.bfloat16)).reshape(k // 32, 32, n)
    amax = np.abs(w).max(1)
    byte = np.clip(np.where(amax > 0, np.frexp(amax)[1] - 1 + 127 - 7, 1), 1, 254)
    scaled = (w * np.exp2(127.0 - byte)[:, None, :]).reshape(k, n).astype(np.float32)
    words = np.ascontiguousarray(scaled.reshape(k // 512, 128, 4, n).transpose(0, 1, 3, 2)).astype(ml_dtypes.float8_e4m3fn).view(np.uint8)
    return words, np.ascontiguousarray(byte.astype(np.uint8).reshape(k // 512, 16, n))


def unpack_weight(words, scales):
    g, p, n, _ = words.shape
    vals = np.ascontiguousarray(words).view(ml_dtypes.float8_e4m3fn).astype(np.float64) * np.repeat(np.exp2(scales.astype(np.float64) - 127.0), 8, axis=1)[..., None]
    return vals.transpose(0, 1, 3, 2).reshape(g * 512, n)

def planes(y):
    n, m = y.shape
    v = y.astype(np.float32).astype(ml_dtypes.bfloat16).astype(np.float64).reshape(n // 32, 32, m)
    top = np.abs(v).max(1)
    byte = np.clip(np.where(top > 0, np.frexp(top)[1] - 1 + 127 - 7, 1), 1, 254)
    codes = (v * np.exp2(127.0 - byte)[:, None, :]).reshape(n, m).astype(np.float32).astype(ml_dtypes.float8_e4m3fn).view(np.uint8)
    words = codes.reshape(n // 512, 128, 4, m).transpose(0, 1, 3, 2)
    return np.ascontiguousarray(words), np.ascontiguousarray(byte.astype(np.uint8).reshape(n // 512, 16, m))


K, T, S, V, H, W, G = 512, 2048, 512, 512, 512, 384, 2048


def setup_inputs():
    n = np.random.standard_normal
    s = mx_kscale(K)[:, None]
    u = mx_kscale(S)
    packed_xT = pack_weight(n((K, T)) * s)
    packed_w1 = pack_weight(n((K, H)) / np.sqrt(K) / s)
    packed_w2 = pack_weight(n((K, H)) / np.sqrt(K) / s)
    return {
        "x_words": packed_xT[0],
        "x_scales": packed_xT[1],
        "w1_words": packed_w1[0],
        "w1_scales": packed_w1[1],
        "w2_words": packed_w2[0],
        "w2_scales": packed_w2[1],
        "ga": (np.random.uniform(0.5, 1.5, (H, 1)) * u[:, None]).astype(np.float32),
        "gb": (np.random.uniform(0.5, 1.5, (H, 1)) / u[:, None]).astype(np.float32),
        "offs": striped8(np.random.randint(0, T, (8, S))),
        "two": striped(np.random.permutation(T)[:V]),
        "n1": striped(np.random.permutation(S)[:W]),
        "n2": striped(np.random.permutation(S)[:W]),
        "n3": striped8(np.stack([np.random.permutation(V) for _ in range(8)])),
        "n4": striped8(np.stack([np.random.permutation(V) for _ in range(8)])),
        "n5": striped(np.random.randint(0, V, G)),
    }


def reference(x_words, x_scales, w1_words, w1_scales, w2_words, w2_scales, ga, gb, offs, two, n1, n2, n3, n4, n5):
    xq = unpack_weight(x_words, x_scales)[np.arange(K)[:, None], runs(offs, K)]
    a = unpack_weight(w1_words, w1_scales).T @ xq
    old = a[:, unstriped(n1)]
    pa = a[:, unstriped(n2)]
    ra = old - np.tanh(pa)
    ds = a.copy()
    ds[:, unstriped(n1)] = ra
    z = f64(ga) * ds
    x_two = unpack_weight(x_words, x_scales)[:, unstriped(two)]
    b = unpack_weight(w2_words, w2_scales).T @ x_two
    z2 = f64(gb) * ((b[np.arange(H)[:, None], runs(n3, H)]) * (b[np.arange(H)[:, None], runs(n4, H)]))
    s = 0.0625 * ((mxq(z, 0, "e4m3").T @ mxq(z2, 0, "e4m3")))
    mb = s[:, unstriped(n5)]
    mx = mb.reshape(S, V, 4).max(axis=2)
    out_0 = s - mx
    return (out_0,) + planes(out_0)

@@ -1,0 +1,282 @@
+from contextlib import ExitStack
+
+import concourse.mybir as mybir
+
+F32 = mybir.dt.float32
+BF16 = mybir.dt.bfloat16
+I32 = mybir.dt.int32
+U32 = mybir.dt.uint32
+U16 = mybir.dt.uint16
+U8 = mybir.dt.uint8
+FP8X4 = mybir.dt.float8_e4m3fn_x4
+ALU = mybir.AluOpType
+ACT = mybir.ActivationFunctionType
+
+P = 128
+PACK = 4
+T = 2048
+N = 512
+W = 384
+CHUNK = 128
+SPARE = 16
+FLOPS = 3 * 2 * 512 * 512 * 512
+
+
+def tile_picked_hkqktanhprodgmaxd_none_po_kernel(
+    tc, x_words, x_scales, w1_words, w1_scales, w2_words, w2_scales, ga, gb, offs, two, n1, n2, n3, n4, n5, out_0, out_1, out_2
+):
+    nc = tc.nc
+    with ExitStack() as ctx:
+        keep = ctx.enter_context(tc.tile_pool(name="keep", bufs=1))
+        psum = ctx.enter_context(tc.psum_pool(name="psum", bufs=1))
+
+        def tile(shape, dtype, name):
+            return keep.tile(shape, dtype, name=name, align_bytes=64)
+
+        def load_list(src, name):
+            lst = tile(list(src.shape), U16, name)
+            nc.sync.dma_start(out=lst[:], in_=src)
+            return lst
+
+        def load_words(queue, src, name):
+            words = tile([P, src.shape[2]], U32, name)
+            queue.dma_start(out=words[:].bitcast(I32), in_=src[0].rearrange("p n t -> p (n t)").bitcast(I32))
+            return words
+
+        def load_scales(queue, src, name):
+            plane = tile([P, src.shape[2]], U8, name)
+            rows = src[0].bitcast(I32)
+            for q in range(4):
+                four = rows[4 * q : 4 * q + 4, :].unsqueeze(0).to_broadcast([8, 4, rows.shape[1]])
+                queue.dma_start(out=plane[32 * q : 32 * q + 32, :].bitcast(I32), in_=four)
+            return plane
+
+        def deal_words(engine, words, name):
+            dealt = tile([P, N], U32, name)
+            engine.tensor_copy(
+                out=dealt[:].bitcast(I32).rearrange("p (t c i) -> p c t i", t=PACK, i=4),
+                in_=words[:].bitcast(I32).rearrange("p (c i t) -> p c t i", t=PACK, i=4),
+            )
+            return dealt
+
+        def deal_plane(engine, plane, name):
+            dealt = tile([P, N], U8, name)
+            engine.tensor_copy(
+                out=dealt[:].rearrange("p (t c i) -> p c t i", t=PACK, i=16),
+                in_=plane[:].rearrange("p (c i t) -> p c t i", t=PACK, i=16),
+            )
+            return dealt
+
+        def product(lhs_words, lhs_plane, rhs_words, rhs_plane, t, bank):
+            acc = psum.tile([P, N], F32, name="acc", tag="bank%d" % bank)
+            cols = slice(t * P, (t + 1) * P)
+            nc.tensor.matmul_mx(
+                out=acc[:],
+                lhsT=lhs_words[:, cols].bitcast(FP8X4),
+                lhsT_scale=lhs_plane[:, cols],
+                rhs=rhs_words[:].bitcast(FP8X4),
+                rhs_scale=rhs_plane[:],
+                start=True,
+                stop=True,
+            )
+            return acc
+
+        def move(on_vector, out, in_):
+            if on_vector:
+                nc.vector.tensor_copy(out=out, in_=in_)
+            else:
+                nc.scalar.activation(out=out, in_=in_, func=ACT.Copy)
+
+        def weigh(on_vector, out, in_, weight):
+            if on_vector:
+                nc.vector.tensor_scalar(out=out, in0=in_, scalar1=weight, scalar2=None, op0=ALU.mult)
+            else:
+                nc.scalar.activation(out=out, in_=in_, func=ACT.Copy, scale=weight)
+
+        two_l = load_list(two, "two_l")
+        x_plane = load_scales(nc.scalar, x_scales, "x_plane")
+        offs_l = load_list(offs, "offs_l")
+        w2_raw = load_words(nc.sync, w2_words, "w2_raw")
+        x_raw = load_words(nc.sync, x_words, "x_raw")
+        w2_raw_plane = load_scales(nc.scalar, w2_scales, "w2_raw_plane")
+        w1_raw_plane = load_scales(nc.gpsimd, w1_scales, "w1_raw_plane")
+        w1_raw = load_words(nc.sync, w1_words, "w1_raw")
+        n3_l = load_list(n3, "n3_l")
+        n4_l = load_list(n4, "n4_l")
+        n2_l = load_list(n2, "n2_l")
+        n1_l = load_list(n1, "n1_l")
+        n5_l = load_list(n5, "n5_l")
+        gb_t = tile([P, PACK], F32, "gb_t")
+        nc.gpsimd.dma_start(out=gb_t[:], in_=gb.rearrange("(p t) o -> p (t o)", t=PACK))
+        ga_t = tile([P, PACK], F32, "ga_t")
+        nc.gpsimd.dma_start(out=ga_t[:], in_=ga.rearrange("(p t) o -> p (t o)", t=PACK))
+
+        two_plane = tile([P, N], U8, "two_plane")
+        nc.vector.tensor_copy(out=two_plane[:], in_=x_plane[:].indirect(two_l[:]))
+        offs_rows = tile([P, N], U8, "offs_rows")
+        nc.vector.tensor_copy(out=offs_rows[:], in_=x_plane[:].indirect(offs_l[:]))
+        offs_plane = tile([P, N], U8, "offs_plane")
+        nc.vector.tensor_copy(out=offs_plane[:].bitcast(I32), in_=offs_rows[:].bitcast(I32))
+        for j in (2, 3):
+            nc.sync.dma_start(out=offs_plane[j:P:32, :].bitcast(I32), in_=offs_rows[16 + j : P : 32, :].bitcast(I32))
+        w2_w = deal_words(nc.vector, w2_raw, "w2_w")
+        w2_p = deal_plane(nc.vector, w2_raw_plane, "w2_p")
+        two_words = tile([P, N], U32, "two_words")
+        nc.vector.tensor_copy(out=two_words[:], in_=x_raw[:].indirect(two_l[:]))
+        offs_words = tile([P, N], U32, "offs_words")
+        nc.vector.tensor_copy(out=offs_words[:], in_=x_raw[:].indirect(offs_l[:]))
+        w1_w = deal_words(nc.vector, w1_raw, "w1_w")
+        w1_p = deal_plane(nc.vector, w1_raw_plane, "w1_p")
+
+        halves = [(slice(h * 256, (h + 1) * 256), slice(h * 16, (h + 1) * 16)) for h in range(2)]
+        z2_rows = tile([P, PACK, N], BF16, "z2_rows")
+        z_rows = tile([P, PACK, N], BF16, "z_rows")
+        b, b3, prod, a, neg_tanh, ds, picked, old, ra = {}, {}, {}, {}, {}, {}, {}, {}, {}
+
+        def evac_b(t):
+            acc = product(w2_w, w2_p, two_words, two_plane, t, t)
+            b[t] = tile([P, N], F32, "b%d" % t)
+            nc.scalar.activation(out=b[t][:], in_=acc[:], func=ACT.Copy)
+
+        def fetch_b3(t, on_vector):
+            b3[t] = tile([P, N], F32, "b3_%d" % t)
+            for cols, lcols in halves:
+                move(on_vector, b3[t][:, cols], b[t][:].indirect(n3_l[:, lcols]))
+
+        def times_b4(t):
+            prod[t] = tile([P, N], F32, "prod%d" % t)
+            for cols, lcols in halves:
+                nc.vector.tensor_tensor(out=prod[t][:, cols], in0=b[t][:].indirect(n4_l[:, lcols]), in1=b3[t][:, cols], op=ALU.mult)
+
+        def weigh_z2(t, on_vector):
+            weigh(on_vector, z2_rows[:, t, :], prod[t][:], gb_t[:, t : t + 1])
+
+        def evac_a(t):
+            acc = product(w1_w, w1_p, offs_words, offs_plane, t, PACK + t)
+            a[t] = tile([P, N], F32, "a%d" % t)
+            nc.scalar.activation(out=a[t][:], in_=acc[:], func=ACT.Copy)
+            neg_tanh[t] = tile([P, N], F32, "neg_tanh%d" % t)
+            nc.scalar.activation(out=neg_tanh[t][:], in_=acc[:], func=ACT.Tanh, scale=-1.0)
+            ds[t] = tile([P, N], F32, "ds%d" % t)
+            nc.sync.dma_start(out=ds[t][:, :N], in_=a[t][:])
+
+        def pick(t):
+            picked[t] = tile([P, W], F32, "picked%d" % t)
+            move(False, picked[t][:], neg_tanh[t][:].indirect(n2_l[:]))
+
+        def fetch_old(t):
+            old[t] = tile([P, W], F32, "old%d" % t)
+            move(False, old[t][:], a[t][:].indirect(n1_l[:]))
+
+        def scatter_sum(t):
+            nc.vector.tensor_tensor(out=ds[t][:].indirect(n1_l[:]), in0=old[t][:], in1=picked[t][:], op=ALU.add)
+
+        def add_old(t):
+            ra[t] = tile([P, W], F32, "ra%d" % t)
+            nc.vector.tensor_tensor(out=ra[t][:], in0=a[t][:].indirect(n1_l[:]), in1=picked[t][:], op=ALU.add)
+
+        def scatter(t, on_vector):
+            move(on_vector, ds[t][:].indirect(n1_l[:]), ra[t][:])
+
+        def weigh_z(t, on_vector):
+            weigh(on_vector, z_rows[:, t, :], ds[t][:, :N], ga_t[:, t : t + 1])
+
+        z2_words = tile([P, N], U32, "z2_words")
+        z2_plane = tile([P, N], U8, "z2_plane")
+        z2_packed = tile([P, N, PACK], BF16, "z2_packed")
+
+        def pack_z2():
+            nc.vector.tensor_copy(
+                out=z2_packed[:].rearrange("p (c i) t -> p c t i", i=4), in_=z2_rows[:].rearrange("p t (c i) -> p c t i", i=4)
+            )
+
+        def quantise_z2():
+            nc.vector.quantize_mx(out=z2_words[:].bitcast(FP8X4), scales=z2_plane[:], in_=z2_packed[:].rearrange("p n t -> p (n t)"))
+
+        for t in range(4):
+            evac_b(t)
+        fetch_b3(0, True)
+        fetch_b3(1, False)
+        evac_a(0)
+        evac_a(1)
+        times_b4(0)
+        times_b4(1)
+        pick(0)
+        pick(1)
+        fetch_b3(2, False)
+        add_old(0)
+        add_old(1)
+        scatter(0, True)
+        evac_a(2)
+        evac_a(3)
+        fetch_b3(3, False)
+        times_b4(2)
+        times_b4(3)
+        pick(2)
+        pick(3)
+        scatter(1, False)
+        for t in range(4):
+            weigh_z2(t, True)
+        weigh_z(0, True)
+        add_old(3)
+        add_old(2)
+        pack_z2()
+        scatter(3, False)
+        quantise_z2()
+        scatter(2, True)
+        weigh_z(1, True)
+        weigh_z(2, True)
+        weigh_z(3, False)
+
+        z_words = tile([P, N], U32, "z_words")
+        z_plane = tile([P, N], U8, "z_plane")
+        s_tiles = []
+        for u in range(PACK):
+            z_packed = tile([P, P, PACK], BF16, "z_packed%d" % u)
+            src = z_rows[:].rearrange("p t (m u) -> p u m t", u=PACK)[:, u]
+            if u != 1:
+                nc.vector.tensor_copy(out=z_packed[:], in_=src)
+            else:
+                nc.scalar.copy(out=z_packed[:], in_=src)
+            cols = slice(u * P, (u + 1) * P)
+            nc.vector.quantize_mx(out=z_words[:, cols].bitcast(FP8X4), scales=z_plane[:, cols], in_=z_packed[:].rearrange("p m t -> p (m t)"))
+            acc = product(z_words, z_plane, z2_words, z2_plane, u, u)
+            s = tile([P, N + SPARE], F32, "s%d" % u)
+            nc.gpsimd.memset(s[:, N:], 0.0)
+            if u != 1:
+                nc.scalar.activation(out=s[:, :N], in_=acc[:], func=ACT.Copy, scale=0.0625)
+            else:
+                nc.vector.tensor_scalar(out=s[:, :N], in0=acc[:], scalar1=0.0625, scalar2=None, op0=ALU.mult)
+            s_tiles.append(s)
+
+        out_words = tile([P, N], U32, "out_words")
+        out_plane = tile([P, N], U8, "out_plane")
+        out_rows = out_0.rearrange("(p u) v -> p u v", u=PACK)
+        words_hbm = out_1[0].rearrange("p n t -> p (n t)").bitcast(I32)
+        for c in range(N // CHUNK):
+            cols = slice(c * CHUNK, (c + 1) * CHUNK)
+            lcols = slice(c * 32, (c + 1) * 32)
+            res = tile([P, PACK, CHUNK], F32, "res%d" % c)
+            for g, us in enumerate(([[(0, 1), (2, 3)]] * 4)[c]):
+                k = len(us)
+                name = "%d_%d" % (c, g)
+                members = keep.tile([P, k, 4 * CHUNK], F32, name="members" + name, tag="members", bufs=8, align_bytes=64)
+                for i, u in enumerate(us):
+                    move((c, u) in ((0, 1), (1, 1), (2, 1), (3, 1)), members[:, i, :], s_tiles[u][:].indirect(n5_l[:, lcols]))
+                quads = members[:].rearrange("p u (v e) -> p (u v) e", e=4)
+                pairs = tile([P, k * CHUNK, 2], F32, "pairs" + name)
+                nc.vector.tensor_tensor(out=pairs[:], in0=quads[:, :, 0:2], in1=quads[:, :, 2:4], op=ALU.max)
+                largest = tile([P, k, CHUNK], F32, "largest" + name)
+                nc.vector.tensor_tensor(out=largest[:].rearrange("p u v -> p (u v)"), in0=pairs[:, :, 0], in1=pairs[:, :, 1], op=ALU.max)
+                for i, u in enumerate(us):
+                    nc.vector.tensor_tensor(out=res[:, u, :], in0=s_tiles[u][:, cols], in1=largest[:, i, :], op=ALU.subtract)
+            nc.sync.dma_start(out=out_rows[:, :, cols], in_=res[:])
+            res_packed = tile([P, CHUNK, PACK], BF16, "res_packed%d" % c)
+            nc.vector.tensor_copy(
+                out=res_packed[:].rearrange("p (c i) t -> p c t i", i=4), in_=res[:].rearrange("p t (c i) -> p c t i", i=4)
+            )
+            nc.vector.quantize_mx(out=out_words[:, cols].bitcast(FP8X4), scales=out_plane[:, cols], in_=res_packed[:].rearrange("p n t -> p (n t)"))
+            nc.sync.dma_start(out=words_hbm[:, cols], in_=out_words[:, cols].bitcast(I32))
+        scale_rows = out_2[0].bitcast(I32)
+        for j in range(4):
+            (nc.sync if j % 2 == 0 else nc.scalar).dma_start(out=scale_rows[j:16:4, :], in_=out_plane[j:P:32, :].bitcast(I32))

@@ -43,12 +43,12 @@ def tile_picked_hkqktanhprodgmaxd_none_po_kernel(
             queue.dma_start(out=words[:].bitcast(I32), in_=src[0].rearrange("p n t -> p (n t)").bitcast(I32))
             return words
 
-        def load_scales(queue, src, name):
+        def load_scales(queues, src, name):
             plane = tile([P, src.shape[2]], U8, name)
             rows = src[0].bitcast(I32)
             for q in range(4):
                 four = rows[4 * q : 4 * q + 4, :].unsqueeze(0).to_broadcast([8, 4, rows.shape[1]])
-                queue.dma_start(out=plane[32 * q : 32 * q + 32, :].bitcast(I32), in_=four)
+                queues[q].dma_start(out=plane[32 * q : 32 * q + 32, :].bitcast(I32), in_=four)
             return plane
 
         def deal_words(engine, words, name):
@@ -94,22 +94,13 @@ def tile_picked_hkqktanhprodgmaxd_none_po_kernel(
                 nc.scalar.activation(out=out, in_=in_, func=ACT.Copy, scale=weight)
 
         two_l = load_list(two, "two_l")
-        x_plane = load_scales(nc.scalar, x_scales, "x_plane")
         offs_l = load_list(offs, "offs_l")
-        w2_raw = load_words(nc.sync, w2_words, "w2_raw")
+        x_plane = load_scales((nc.sync,) * 4, x_scales, "x_plane")
         x_raw = load_words(nc.sync, x_words, "x_raw")
-        w2_raw_plane = load_scales(nc.scalar, w2_scales, "w2_raw_plane")
-        w1_raw_plane = load_scales(nc.gpsimd, w1_scales, "w1_raw_plane")
+        w2_raw = load_words(nc.sync, w2_words, "w2_raw")
+        w2_raw_plane = load_scales((nc.sync,) * 4, w2_scales, "w2_raw_plane")
         w1_raw = load_words(nc.sync, w1_words, "w1_raw")
         n3_l = load_list(n3, "n3_l")
-        n4_l = load_list(n4, "n4_l")
-        n2_l = load_list(n2, "n2_l")
-        n1_l = load_list(n1, "n1_l")
-        n5_l = load_list(n5, "n5_l")
-        gb_t = tile([P, PACK], F32, "gb_t")
-        nc.gpsimd.dma_start(out=gb_t[:], in_=gb.rearrange("(p t) o -> p (t o)", t=PACK))
-        ga_t = tile([P, PACK], F32, "ga_t")
-        nc.gpsimd.dma_start(out=ga_t[:], in_=ga.rearrange("(p t) o -> p (t o)", t=PACK))
 
         two_plane = tile([P, N], U8, "two_plane")
         nc.vector.tensor_copy(out=two_plane[:], in_=x_plane[:].indirect(two_l[:]))
@@ -119,6 +110,15 @@ def tile_picked_hkqktanhprodgmaxd_none_po_kernel(
         nc.vector.tensor_copy(out=offs_plane[:].bitcast(I32), in_=offs_rows[:].bitcast(I32))
         for j in (2, 3):
             nc.sync.dma_start(out=offs_plane[j:P:32, :].bitcast(I32), in_=offs_rows[16 + j : P : 32, :].bitcast(I32))
+        w1_raw_plane = load_scales((nc.sync,) * 4, w1_scales, "w1_raw_plane")
+        n4_l = load_list(n4, "n4_l")
+        n2_l = load_list(n2, "n2_l")
+        n1_l = load_list(n1, "n1_l")
+        gb_t = tile([P, PACK], F32, "gb_t")
+        nc.sync.dma_start(out=gb_t[:], in_=gb.rearrange("(p t) o -> p (t o)", t=PACK))
+        ga_t = tile([P, PACK], F32, "ga_t")
+        nc.sync.dma_start(out=ga_t[:], in_=ga.rearrange("(p t) o -> p (t o)", t=PACK))
+        n5_l = load_list(n5, "n5_l")
         w2_w = deal_words(nc.vector, w2_raw, "w2_w")
         w2_p = deal_plane(nc.vector, w2_raw_plane, "w2_p")
         two_words = tile([P, N], U32, "two_words")
@@ -128,52 +128,48 @@ def tile_picked_hkqktanhprodgmaxd_none_po_kernel(
         w1_w = deal_words(nc.vector, w1_raw, "w1_w")
         w1_p = deal_plane(nc.vector, w1_raw_plane, "w1_p")
 
-        halves = [(slice(h * 256, (h + 1) * 256), slice(h * 16, (h + 1) * 16)) for h in range(2)]
         z2_rows = tile([P, PACK, N], BF16, "z2_rows")
         z_rows = tile([P, PACK, N], BF16, "z_rows")
         b, b3, prod, a, neg_tanh, ds, picked, old, ra = {}, {}, {}, {}, {}, {}, {}, {}, {}
 
-        def evac_b(t):
+        def evac_b(t, on_vector):
             acc = product(w2_w, w2_p, two_words, two_plane, t, t)
-            b[t] = tile([P, N], F32, "b%d" % t)
-            nc.scalar.activation(out=b[t][:], in_=acc[:], func=ACT.Copy)
+            b[t] = tile([P, 2 * N], F32, "b%d" % t)
+            nc.vector.memset(b[t][:, N:], 0.0)
+            move(on_vector, b[t][:, :N], acc[:])
 
-        def fetch_b3(t, on_vector):
+        def fetch_b3(t):
             b3[t] = tile([P, N], F32, "b3_%d" % t)
-            for cols, lcols in halves:
-                move(on_vector, b3[t][:, cols], b[t][:].indirect(n3_l[:, lcols]))
+            nc.scalar.activation(out=b3[t][:], in_=b[t][:].indirect(n3_l[:]), func=ACT.Copy)
 
         def times_b4(t):
             prod[t] = tile([P, N], F32, "prod%d" % t)
-            for cols, lcols in halves:
-                nc.vector.tensor_tensor(out=prod[t][:, cols], in0=b[t][:].indirect(n4_l[:, lcols]), in1=b3[t][:, cols], op=ALU.mult)
-
-        def weigh_z2(t, on_vector):
-            weigh(on_vector, z2_rows[:, t, :], prod[t][:], gb_t[:, t : t + 1])
+            nc.vector.tensor_tensor(out=prod[t][:], in0=b[t][:].indirect(n4_l[:]), in1=b3[t][:], op=ALU.mult)
+            weigh(t in (0, 1, 2, 3), z2_rows[:, t, :], prod[t][:], gb_t[:, t : t + 1])
 
         def evac_a(t):
             acc = product(w1_w, w1_p, offs_words, offs_plane, t, PACK + t)
             a[t] = tile([P, N], F32, "a%d" % t)
             nc.scalar.activation(out=a[t][:], in_=acc[:], func=ACT.Copy)
-            neg_tanh[t] = tile([P, N], F32, "neg_tanh%d" % t)
-            nc.scalar.activation(out=neg_tanh[t][:], in_=acc[:], func=ACT.Tanh, scale=-1.0)
-            ds[t] = tile([P, N], F32, "ds%d" % t)
+            ds[t] = tile([P, 2 * W], F32, "ds%d" % t)
             nc.sync.dma_start(out=ds[t][:, :N], in_=a[t][:])
 
         def pick(t):
             picked[t] = tile([P, W], F32, "picked%d" % t)
-            move(False, picked[t][:], neg_tanh[t][:].indirect(n2_l[:]))
+            move(False, picked[t][:], a[t][:].indirect(n2_l[:]))
+            neg_tanh[t] = tile([P, W], F32, "neg_tanh%d" % t)
+            nc.scalar.activation(out=neg_tanh[t][:], in_=picked[t][:], func=ACT.Tanh, scale=-1.0)
 
         def fetch_old(t):
             old[t] = tile([P, W], F32, "old%d" % t)
             move(False, old[t][:], a[t][:].indirect(n1_l[:]))
 
         def scatter_sum(t):
-            nc.vector.tensor_tensor(out=ds[t][:].indirect(n1_l[:]), in0=old[t][:], in1=picked[t][:], op=ALU.add)
+            nc.vector.tensor_tensor(out=ds[t][:].indirect(n1_l[:]), in0=old[t][:], in1=neg_tanh[t][:], op=ALU.add)
 
         def add_old(t):
             ra[t] = tile([P, W], F32, "ra%d" % t)
-            nc.vector.tensor_tensor(out=ra[t][:], in0=a[t][:].indirect(n1_l[:]), in1=picked[t][:], op=ALU.add)
+            nc.vector.tensor_tensor(out=ra[t][:], in0=a[t][:].indirect(n1_l[:]), in1=neg_tanh[t][:], op=ALU.add)
 
         def scatter(t, on_vector):
             move(on_vector, ds[t][:].indirect(n1_l[:]), ra[t][:])
@@ -194,39 +190,26 @@ def tile_picked_hkqktanhprodgmaxd_none_po_kernel(
             nc.vector.quantize_mx(out=z2_words[:].bitcast(FP8X4), scales=z2_plane[:], in_=z2_packed[:].rearrange("p n t -> p (n t)"))
 
         for t in range(4):
-            evac_b(t)
-        fetch_b3(0, True)
-        fetch_b3(1, False)
-        evac_a(0)
-        evac_a(1)
-        times_b4(0)
-        times_b4(1)
-        pick(0)
-        pick(1)
-        fetch_b3(2, False)
-        add_old(0)
-        add_old(1)
-        scatter(0, True)
-        evac_a(2)
-        evac_a(3)
-        fetch_b3(3, False)
-        times_b4(2)
-        times_b4(3)
-        pick(2)
-        pick(3)
-        scatter(1, False)
+            evac_b(t, t > 0)
         for t in range(4):
-            weigh_z2(t, True)
-        weigh_z(0, True)
-        add_old(3)
-        add_old(2)
+            fetch_b3(t)
+            times_b4(t)
         pack_z2()
-        scatter(3, False)
         quantise_z2()
-        scatter(2, True)
-        weigh_z(1, True)
-        weigh_z(2, True)
-        weigh_z(3, False)
+        for pair in ((0, 1), (2, 3)):
+            for t in pair:
+                evac_a(t)
+            for t in pair:
+                pick(t)
+            for t in pair:
+                (fetch_old if t in (2,) else add_old)(t)
+        for t in range(4):
+            if t in (2,):
+                scatter_sum(t)
+            else:
+                scatter(t, t in (0, 2))
+        for t in range(4):
+            weigh_z(t, t in (1, 3))
 
         z_words = tile([P, N], U32, "z_words")
         z_plane = tile([P, N], U8, "z_plane")
@@ -234,20 +217,33 @@ def tile_picked_hkqktanhprodgmaxd_none_po_kernel(
         for u in range(PACK):
             z_packed = tile([P, P, PACK], BF16, "z_packed%d" % u)
             src = z_rows[:].rearrange("p t (m u) -> p u m t", u=PACK)[:, u]
-            if u != 1:
+            if u not in (1,):
                 nc.vector.tensor_copy(out=z_packed[:], in_=src)
             else:
                 nc.scalar.copy(out=z_packed[:], in_=src)
             cols = slice(u * P, (u + 1) * P)
             nc.vector.quantize_mx(out=z_words[:, cols].bitcast(FP8X4), scales=z_plane[:, cols], in_=z_packed[:].rearrange("p m t -> p (m t)"))
             acc = product(z_words, z_plane, z2_words, z2_plane, u, u)
-            s = tile([P, N + SPARE], F32, "s%d" % u)
-            nc.gpsimd.memset(s[:, N:], 0.0)
-            if u != 1:
+            s = tile([P, (2 * N if u == 0 else N) + SPARE], F32, "s%d" % u)
+            nc.vector.memset(s[:, N:], 0.0)
+            if u != 0:
                 nc.scalar.activation(out=s[:, :N], in_=acc[:], func=ACT.Copy, scale=0.0625)
             else:
                 nc.vector.tensor_scalar(out=s[:, :N], in0=acc[:], scalar1=0.0625, scalar2=None, op0=ALU.mult)
             s_tiles.append(s)
+
+        def largest_of_four(members, width, name):
+            quads = members.rearrange("p (v e) -> p v e", e=4)
+            pairs = tile([P, width, 2], F32, "pairs" + name)
+            nc.vector.tensor_tensor(out=pairs[:], in0=quads[:, :, 0:2], in1=quads[:, :, 2:4], op=ALU.max)
+            largest = tile([P, width], F32, "largest" + name)
+            nc.vector.tensor_tensor(out=largest[:], in0=pairs[:, :, 0], in1=pairs[:, :, 1], op=ALU.max)
+            return largest
+
+        own_members = tile([P, 4 * N], F32, "own_members")
+        for h in range(2):
+            move(True, own_members[:, h * 2 * N : (h + 1) * 2 * N], s_tiles[0][:].indirect(n5_l[:, h * 64 : (h + 1) * 64]))
+        own_largest = largest_of_four(own_members[:], N, "_own")
 
         out_words = tile([P, N], U32, "out_words")
         out_plane = tile([P, N], U8, "out_plane")
@@ -257,19 +253,15 @@ def tile_picked_hkqktanhprodgmaxd_none_po_kernel(
             cols = slice(c * CHUNK, (c + 1) * CHUNK)
             lcols = slice(c * 32, (c + 1) * 32)
             res = tile([P, PACK, CHUNK], F32, "res%d" % c)
-            for g, us in enumerate(([[(0, 1), (2, 3)]] * 4)[c]):
-                k = len(us)
+            nc.vector.tensor_tensor(out=res[:, 0, :], in0=s_tiles[0][:, cols], in1=own_largest[:, cols], op=ALU.subtract)
+            for g, us in enumerate(([[(1, 2, 3)]] * 3 + [[(1, 2), (3,)]])[c]):
                 name = "%d_%d" % (c, g)
-                members = keep.tile([P, k, 4 * CHUNK], F32, name="members" + name, tag="members", bufs=8, align_bytes=64)
+                members = tile([P, len(us), 4 * CHUNK], F32, "members" + name)
                 for i, u in enumerate(us):
-                    move((c, u) in ((0, 1), (1, 1), (2, 1), (3, 1)), members[:, i, :], s_tiles[u][:].indirect(n5_l[:, lcols]))
-                quads = members[:].rearrange("p u (v e) -> p (u v) e", e=4)
-                pairs = tile([P, k * CHUNK, 2], F32, "pairs" + name)
-                nc.vector.tensor_tensor(out=pairs[:], in0=quads[:, :, 0:2], in1=quads[:, :, 2:4], op=ALU.max)
-                largest = tile([P, k, CHUNK], F32, "largest" + name)
-                nc.vector.tensor_tensor(out=largest[:].rearrange("p u v -> p (u v)"), in0=pairs[:, :, 0], in1=pairs[:, :, 1], op=ALU.max)
+                    move(False, members[:, i, :], s_tiles[u][:].indirect(n5_l[:, lcols]))
+                largest = largest_of_four(members[:].rearrange("p u e -> p (u e)"), len(us) * CHUNK, name)
                 for i, u in enumerate(us):
-                    nc.vector.tensor_tensor(out=res[:, u, :], in0=s_tiles[u][:, cols], in1=largest[:, i, :], op=ALU.subtract)
+                    nc.vector.tensor_tensor(out=res[:, u, :], in0=s_tiles[u][:, cols], in1=largest[:, i * CHUNK : (i + 1) * CHUNK], op=ALU.subtract)
             nc.sync.dma_start(out=out_rows[:, :, cols], in_=res[:])
             res_packed = tile([P, CHUNK, PACK], BF16, "res_packed%d" % c)
             nc.vector.tensor_copy(

@@ -30,8 +30,8 @@ def tile_picked_hkqktanhprodgmaxd_none_po_kernel(
         keep = ctx.enter_context(tc.tile_pool(name="keep", bufs=1))
         psum = ctx.enter_context(tc.psum_pool(name="psum", bufs=1))
 
-        def tile(shape, dtype, name):
-            return keep.tile(shape, dtype, name=name, align_bytes=64)
+        def tile(shape, dtype, name, tag=None):
+            return keep.tile(shape, dtype, name=name, tag=tag or name, align_bytes=64)
 
         def load_list(src, name):
             lst = tile(list(src.shape), U16, name)
@@ -43,8 +43,8 @@ def tile_picked_hkqktanhprodgmaxd_none_po_kernel(
             queue.dma_start(out=words[:].bitcast(I32), in_=src[0].rearrange("p n t -> p (n t)").bitcast(I32))
             return words
 
-        def load_scales(queues, src, name):
-            plane = tile([P, src.shape[2]], U8, name)
+        def load_scales(queues, src, name, tag=None):
+            plane = tile([P, src.shape[2]], U8, name, tag)
             rows = src[0].bitcast(I32)
             for q in range(4):
                 four = rows[4 * q : 4 * q + 4, :].unsqueeze(0).to_broadcast([8, 4, rows.shape[1]])
@@ -96,9 +96,9 @@ def tile_picked_hkqktanhprodgmaxd_none_po_kernel(
         two_l = load_list(two, "two_l")
         offs_l = load_list(offs, "offs_l")
         x_plane = load_scales((nc.sync,) * 4, x_scales, "x_plane")
-        x_raw = load_words(nc.sync, x_words, "x_raw")
         w2_raw = load_words(nc.sync, w2_words, "w2_raw")
-        w2_raw_plane = load_scales((nc.sync,) * 4, w2_scales, "w2_raw_plane")
+        x_raw = load_words(nc.sync, x_words, "x_raw")
+        w2_raw_plane = load_scales((nc.sync,) * 4, w2_scales, "w2_raw_plane", "shared")
         w1_raw = load_words(nc.sync, w1_words, "w1_raw")
         n3_l = load_list(n3, "n3_l")
 
@@ -123,7 +123,7 @@ def tile_picked_hkqktanhprodgmaxd_none_po_kernel(
         w2_p = deal_plane(nc.vector, w2_raw_plane, "w2_p")
         two_words = tile([P, N], U32, "two_words")
         nc.vector.tensor_copy(out=two_words[:], in_=x_raw[:].indirect(two_l[:]))
-        offs_words = tile([P, N], U32, "offs_words")
+        offs_words = tile([P, N], U32, "offs_words", "shared")
         nc.vector.tensor_copy(out=offs_words[:], in_=x_raw[:].indirect(offs_l[:]))
         w1_w = deal_words(nc.vector, w1_raw, "w1_w")
         w1_p = deal_plane(nc.vector, w1_raw_plane, "w1_p")
@@ -226,7 +226,7 @@ def tile_picked_hkqktanhprodgmaxd_none_po_kernel(
             acc = product(z_words, z_plane, z2_words, z2_plane, u, u)
             s = tile([P, (2 * N if u == 0 else N) + SPARE], F32, "s%d" % u)
             nc.vector.memset(s[:, N:], 0.0)
-            if u != 0:
+            if u not in (0, 3):
                 nc.scalar.activation(out=s[:, :N], in_=acc[:], func=ACT.Copy, scale=0.0625)
             else:
                 nc.vector.tensor_scalar(out=s[:, :N], in0=acc[:], scalar1=0.0625, scalar2=None, op0=ALU.mult)
@@ -249,24 +249,22 @@ def tile_picked_hkqktanhprodgmaxd_none_po_kernel(
         out_plane = tile([P, N], U8, "out_plane")
         out_rows = out_0.rearrange("(p u) v -> p u v", u=PACK)
         words_hbm = out_1[0].rearrange("p n t -> p (n t)").bitcast(I32)
-        for c in range(N // CHUNK):
-            cols = slice(c * CHUNK, (c + 1) * CHUNK)
-            lcols = slice(c * 32, (c + 1) * 32)
-            res = tile([P, PACK, CHUNK], F32, "res%d" % c)
+        for c, (first, CW) in enumerate(((0, 128), (128, 128), (256, 128), (384, 128))):
+            cols = slice(first, first + CW)
+            lcols = slice(first // 4, (first + CW) // 4)
+            res = tile([P, PACK, CW], F32, "res%d" % c)
             nc.vector.tensor_tensor(out=res[:, 0, :], in0=s_tiles[0][:, cols], in1=own_largest[:, cols], op=ALU.subtract)
-            for g, us in enumerate(([[(1, 2, 3)]] * 3 + [[(1, 2), (3,)]])[c]):
+            for g, us in enumerate([(1, 2), (3,)] if c == len(((0, 128), (128, 128), (256, 128), (384, 128))) - 1 else [(1, 2, 3)]):
                 name = "%d_%d" % (c, g)
-                members = tile([P, len(us), 4 * CHUNK], F32, "members" + name)
+                members = tile([P, len(us), 4 * CW], F32, "members" + name)
                 for i, u in enumerate(us):
                     move(False, members[:, i, :], s_tiles[u][:].indirect(n5_l[:, lcols]))
-                largest = largest_of_four(members[:].rearrange("p u e -> p (u e)"), len(us) * CHUNK, name)
+                largest = largest_of_four(members[:].rearrange("p u e -> p (u e)"), len(us) * CW, name)
                 for i, u in enumerate(us):
-                    nc.vector.tensor_tensor(out=res[:, u, :], in0=s_tiles[u][:, cols], in1=largest[:, i * CHUNK : (i + 1) * CHUNK], op=ALU.subtract)
+                    nc.vector.tensor_tensor(out=res[:, u, :], in0=s_tiles[u][:, cols], in1=largest[:, i * CW : (i + 1) * CW], op=ALU.subtract)
             nc.sync.dma_start(out=out_rows[:, :, cols], in_=res[:])
-            res_packed = tile([P, CHUNK, PACK], BF16, "res_packed%d" % c)
-            nc.vector.tensor_copy(
-                out=res_packed[:].rearrange("p (c i) t -> p c t i", i=4), in_=res[:].rearrange("p t (c i) -> p c t i", i=4)
-            )
+            res_packed = tile([P, CW, PACK], BF16, "res_packed%d" % c)
+            move(c not in (2,), res_packed[:].rearrange("p (c i) t -> p c t i", i=4), res[:].rearrange("p t (c i) -> p c t i", i=4))
             nc.vector.quantize_mx(out=out_words[:, cols].bitcast(FP8X4), scales=out_plane[:, cols], in_=res_packed[:].rearrange("p n t -> p (n t)"))
             nc.sync.dma_start(out=words_hbm[:, cols], in_=out_words[:, cols].bitcast(I32))
         scale_rows = out_2[0].bitcast(I32)

from contextlib import ExitStack

import concourse.mybir as mybir

F32 = mybir.dt.float32
BF16 = mybir.dt.bfloat16
I32 = mybir.dt.int32
U32 = mybir.dt.uint32
U16 = mybir.dt.uint16
U8 = mybir.dt.uint8
FP8X4 = mybir.dt.float8_e4m3fn_x4
ALU = mybir.AluOpType
ACT = mybir.ActivationFunctionType

P = 128
PACK = 4
T = 2048
N = 512
W = 384
CHUNK = 128
SPARE = 16
FLOPS = 3 * 2 * 512 * 512 * 512


def tile_picked_hkqktanhprodgmaxd_none_po_kernel(
    tc, x_words, x_scales, w1_words, w1_scales, w2_words, w2_scales, ga, gb, offs, two, n1, n2, n3, n4, n5, out_0, out_1, out_2
):
    nc = tc.nc
    with ExitStack() as ctx:
        keep = ctx.enter_context(tc.tile_pool(name="keep", bufs=1))
        psum = ctx.enter_context(tc.psum_pool(name="psum", bufs=1))

        def tile(shape, dtype, name, tag=None):
            return keep.tile(shape, dtype, name=name, tag=tag or name, align_bytes=64)

        def load_list(src, name):
            lst = tile(list(src.shape), U16, name)
            nc.sync.dma_start(out=lst[:], in_=src)
            return lst

        def load_words(queue, src, name):
            words = tile([P, src.shape[2]], U32, name)
            queue.dma_start(out=words[:].bitcast(I32), in_=src[0].rearrange("p n t -> p (n t)").bitcast(I32))
            return words

        def load_scales(queues, src, name, tag=None):
            plane = tile([P, src.shape[2]], U8, name, tag)
            rows = src[0].bitcast(I32)
            for q in range(4):
                four = rows[4 * q : 4 * q + 4, :].unsqueeze(0).to_broadcast([8, 4, rows.shape[1]])
                queues[q].dma_start(out=plane[32 * q : 32 * q + 32, :].bitcast(I32), in_=four)
            return plane

        def deal_words(engine, words, name):
            dealt = tile([P, N], U32, name)
            engine.tensor_copy(
                out=dealt[:].bitcast(I32).rearrange("p (t c i) -> p c t i", t=PACK, i=4),
                in_=words[:].bitcast(I32).rearrange("p (c i t) -> p c t i", t=PACK, i=4),
            )
            return dealt

        def deal_plane(engine, plane, name):
            dealt = tile([P, N], U8, name)
            engine.tensor_copy(
                out=dealt[:].rearrange("p (t c i) -> p c t i", t=PACK, i=16),
                in_=plane[:].rearrange("p (c i t) -> p c t i", t=PACK, i=16),
            )
            return dealt

        def product(lhs_words, lhs_plane, rhs_words, rhs_plane, t, bank):
            acc = psum.tile([P, N], F32, name="acc", tag="bank%d" % bank)
            cols = slice(t * P, (t + 1) * P)
            nc.tensor.matmul_mx(
                out=acc[:],
                lhsT=lhs_words[:, cols].bitcast(FP8X4),
                lhsT_scale=lhs_plane[:, cols],
                rhs=rhs_words[:].bitcast(FP8X4),
                rhs_scale=rhs_plane[:],
                start=True,
                stop=True,
            )
            return acc

        def move(on_vector, out, in_):
            if on_vector:
                nc.vector.tensor_copy(out=out, in_=in_)
            else:
                nc.scalar.activation(out=out, in_=in_, func=ACT.Copy)

        def weigh(on_vector, out, in_, weight):
            if on_vector:
                nc.vector.tensor_scalar(out=out, in0=in_, scalar1=weight, scalar2=None, op0=ALU.mult)
            else:
                nc.scalar.activation(out=out, in_=in_, func=ACT.Copy, scale=weight)

        two_l = load_list(two, "two_l")
        offs_l = load_list(offs, "offs_l")
        x_plane = load_scales((nc.sync,) * 4, x_scales, "x_plane")
        w2_raw = load_words(nc.sync, w2_words, "w2_raw")
        x_raw = load_words(nc.sync, x_words, "x_raw")
        w2_raw_plane = load_scales((nc.sync,) * 4, w2_scales, "w2_raw_plane", "shared")
        w1_raw = load_words(nc.sync, w1_words, "w1_raw")
        n3_l = load_list(n3, "n3_l")

        two_plane = tile([P, N], U8, "two_plane")
        nc.vector.tensor_copy(out=two_plane[:], in_=x_plane[:].indirect(two_l[:]))
        offs_rows = tile([P, N], U8, "offs_rows")
        nc.vector.tensor_copy(out=offs_rows[:], in_=x_plane[:].indirect(offs_l[:]))
        offs_plane = tile([P, N], U8, "offs_plane")
        nc.vector.tensor_copy(out=offs_plane[:].bitcast(I32), in_=offs_rows[:].bitcast(I32))
        for j in (2, 3):
            nc.sync.dma_start(out=offs_plane[j:P:32, :].bitcast(I32), in_=offs_rows[16 + j : P : 32, :].bitcast(I32))
        w1_raw_plane = load_scales((nc.sync,) * 4, w1_scales, "w1_raw_plane")
        n4_l = load_list(n4, "n4_l")
        n2_l = load_list(n2, "n2_l")
        n1_l = load_list(n1, "n1_l")
        gb_t = tile([P, PACK], F32, "gb_t")
        nc.sync.dma_start(out=gb_t[:], in_=gb.rearrange("(p t) o -> p (t o)", t=PACK))
        ga_t = tile([P, PACK], F32, "ga_t")
        nc.sync.dma_start(out=ga_t[:], in_=ga.rearrange("(p t) o -> p (t o)", t=PACK))
        n5_l = load_list(n5, "n5_l")
        w2_w = deal_words(nc.vector, w2_raw, "w2_w")
        w2_p = deal_plane(nc.vector, w2_raw_plane, "w2_p")
        two_words = tile([P, N], U32, "two_words")
        nc.vector.tensor_copy(out=two_words[:], in_=x_raw[:].indirect(two_l[:]))
        offs_words = tile([P, N], U32, "offs_words", "shared")
        nc.vector.tensor_copy(out=offs_words[:], in_=x_raw[:].indirect(offs_l[:]))
        w1_w = deal_words(nc.vector, w1_raw, "w1_w")
        w1_p = deal_plane(nc.vector, w1_raw_plane, "w1_p")

        z2_rows = tile([P, PACK, N], BF16, "z2_rows")
        z_rows = tile([P, PACK, N], BF16, "z_rows")
        b, b3, prod, a, neg_tanh, ds, picked, old, ra = {}, {}, {}, {}, {}, {}, {}, {}, {}

        def evac_b(t, on_vector):
            acc = product(w2_w, w2_p, two_words, two_plane, t, t)
            b[t] = tile([P, 2 * N], F32, "b%d" % t)
            nc.vector.memset(b[t][:, N:], 0.0)
            move(on_vector, b[t][:, :N], acc[:])

        def fetch_b3(t):
            b3[t] = tile([P, N], F32, "b3_%d" % t)
            nc.scalar.activation(out=b3[t][:], in_=b[t][:].indirect(n3_l[:]), func=ACT.Copy)

        def times_b4(t):
            prod[t] = tile([P, N], F32, "prod%d" % t)
            nc.vector.tensor_tensor(out=prod[t][:], in0=b[t][:].indirect(n4_l[:]), in1=b3[t][:], op=ALU.mult)
            weigh(t in (0, 1, 2, 3), z2_rows[:, t, :], prod[t][:], gb_t[:, t : t + 1])

        def evac_a(t):
            acc = product(w1_w, w1_p, offs_words, offs_plane, t, PACK + t)
            a[t] = tile([P, N], F32, "a%d" % t)
            nc.scalar.activation(out=a[t][:], in_=acc[:], func=ACT.Copy)
            ds[t] = tile([P, 2 * W], F32, "ds%d" % t)
            nc.sync.dma_start(out=ds[t][:, :N], in_=a[t][:])

        def pick(t):
            picked[t] = tile([P, W], F32, "picked%d" % t)
            move(False, picked[t][:], a[t][:].indirect(n2_l[:]))
            neg_tanh[t] = tile([P, W], F32, "neg_tanh%d" % t)
            nc.scalar.activation(out=neg_tanh[t][:], in_=picked[t][:], func=ACT.Tanh, scale=-1.0)

        def fetch_old(t):
            old[t] = tile([P, W], F32, "old%d" % t)
            move(False, old[t][:], a[t][:].indirect(n1_l[:]))

        def scatter_sum(t):
            nc.vector.tensor_tensor(out=ds[t][:].indirect(n1_l[:]), in0=old[t][:], in1=neg_tanh[t][:], op=ALU.add)

        def add_old(t):
            ra[t] = tile([P, W], F32, "ra%d" % t)
            nc.vector.tensor_tensor(out=ra[t][:], in0=a[t][:].indirect(n1_l[:]), in1=neg_tanh[t][:], op=ALU.add)

        def scatter(t, on_vector):
            move(on_vector, ds[t][:].indirect(n1_l[:]), ra[t][:])

        def weigh_z(t, on_vector):
            weigh(on_vector, z_rows[:, t, :], ds[t][:, :N], ga_t[:, t : t + 1])

        z2_words = tile([P, N], U32, "z2_words")
        z2_plane = tile([P, N], U8, "z2_plane")
        z2_packed = tile([P, N, PACK], BF16, "z2_packed")

        def pack_z2():
            nc.vector.tensor_copy(
                out=z2_packed[:].rearrange("p (c i) t -> p c t i", i=4), in_=z2_rows[:].rearrange("p t (c i) -> p c t i", i=4)
            )

        def quantise_z2():
            nc.vector.quantize_mx(out=z2_words[:].bitcast(FP8X4), scales=z2_plane[:], in_=z2_packed[:].rearrange("p n t -> p (n t)"))

        for t in range(4):
            evac_b(t, t > 0)
        for t in range(4):
            fetch_b3(t)
            times_b4(t)
        pack_z2()
        quantise_z2()
        for pair in ((0, 1), (2, 3)):
            for t in pair:
                evac_a(t)
            for t in pair:
                pick(t)
            for t in pair:
                (fetch_old if t in (2,) else add_old)(t)
        for t in range(4):
            if t in (2,):
                scatter_sum(t)
            else:
                scatter(t, t in (0, 2))
        for t in range(4):
            weigh_z(t, t in (1, 3))

        z_words = tile([P, N], U32, "z_words")
        z_plane = tile([P, N], U8, "z_plane")
        s_tiles = []
        for u in range(PACK):
            z_packed = tile([P, P, PACK], BF16, "z_packed%d" % u)
            src = z_rows[:].rearrange("p t (m u) -> p u m t", u=PACK)[:, u]
            if u not in (1,):
                nc.vector.tensor_copy(out=z_packed[:], in_=src)
            else:
                nc.scalar.copy(out=z_packed[:], in_=src)
            cols = slice(u * P, (u + 1) * P)
            nc.vector.quantize_mx(out=z_words[:, cols].bitcast(FP8X4), scales=z_plane[:, cols], in_=z_packed[:].rearrange("p m t -> p (m t)"))
            acc = product(z_words, z_plane, z2_words, z2_plane, u, u)
            s = tile([P, (2 * N if u == 0 else N) + SPARE], F32, "s%d" % u)
            nc.vector.memset(s[:, N:], 0.0)
            if u not in (0, 3):
                nc.scalar.activation(out=s[:, :N], in_=acc[:], func=ACT.Copy, scale=0.0625)
            else:
                nc.vector.tensor_scalar(out=s[:, :N], in0=acc[:], scalar1=0.0625, scalar2=None, op0=ALU.mult)
            s_tiles.append(s)

        def largest_of_four(members, width, name):
            quads = members.rearrange("p (v e) -> p v e", e=4)
            pairs = tile([P, width, 2], F32, "pairs" + name)
            nc.vector.tensor_tensor(out=pairs[:], in0=quads[:, :, 0:2], in1=quads[:, :, 2:4], op=ALU.max)
            largest = tile([P, width], F32, "largest" + name)
            nc.vector.tensor_tensor(out=largest[:], in0=pairs[:, :, 0], in1=pairs[:, :, 1], op=ALU.max)
            return largest

        own_members = tile([P, 4 * N], F32, "own_members")
        for h in range(2):
            move(True, own_members[:, h * 2 * N : (h + 1) * 2 * N], s_tiles[0][:].indirect(n5_l[:, h * 64 : (h + 1) * 64]))
        own_largest = largest_of_four(own_members[:], N, "_own")

        out_words = tile([P, N], U32, "out_words")
        out_plane = tile([P, N], U8, "out_plane")
        out_rows = out_0.rearrange("(p u) v -> p u v", u=PACK)
        words_hbm = out_1[0].rearrange("p n t -> p (n t)").bitcast(I32)
        for c, (first, CW) in enumerate(((0, 128), (128, 128), (256, 128), (384, 128))):
            cols = slice(first, first + CW)
            lcols = slice(first // 4, (first + CW) // 4)
            res = tile([P, PACK, CW], F32, "res%d" % c)
            nc.vector.tensor_tensor(out=res[:, 0, :], in0=s_tiles[0][:, cols], in1=own_largest[:, cols], op=ALU.subtract)
            for g, us in enumerate([(1, 2), (3,)] if c == len(((0, 128), (128, 128), (256, 128), (384, 128))) - 1 else [(1, 2, 3)]):
                name = "%d_%d" % (c, g)
                members = tile([P, len(us), 4 * CW], F32, "members" + name)
                for i, u in enumerate(us):
                    move(False, members[:, i, :], s_tiles[u][:].indirect(n5_l[:, lcols]))
                largest = largest_of_four(members[:].rearrange("p u e -> p (u e)"), len(us) * CW, name)
                for i, u in enumerate(us):
                    nc.vector.tensor_tensor(out=res[:, u, :], in0=s_tiles[u][:, cols], in1=largest[:, i * CW : (i + 1) * CW], op=ALU.subtract)
            nc.sync.dma_start(out=out_rows[:, :, cols], in_=res[:])
            res_packed = tile([P, CW, PACK], BF16, "res_packed%d" % c)
            move(c not in (2,), res_packed[:].rearrange("p (c i) t -> p c t i", i=4), res[:].rearrange("p t (c i) -> p c t i", i=4))
            nc.vector.quantize_mx(out=out_words[:, cols].bitcast(FP8X4), scales=out_plane[:, cols], in_=res_packed[:].rearrange("p n t -> p (n t)"))
            nc.sync.dma_start(out=words_hbm[:, cols], in_=out_words[:, cols].bitcast(I32))
        scale_rows = out_2[0].bitcast(I32)
        for j in range(4):
            (nc.sync if j % 2 == 0 else nc.scalar).dma_start(out=scale_rows[j:16:4, :], in_=out_plane[j:P:32, :].bitcast(I32))
